import numpy as np
import ml_dtypes


def mxq(x, axis, fmt="e4m3"):
    dtype, down = {"e4m3": (ml_dtypes.float8_e4m3fn, 7), "e5m2": (ml_dtypes.float8_e5m2, 14)}[fmt]
    v = np.moveaxis(np.asarray(x, np.float32).astype(ml_dtypes.bfloat16).astype(np.float64), axis, -1)
    blocks = v.reshape(v.shape[:-1] + (-1, 32))
    amax = np.abs(blocks).max(-1, keepdims=True)
    byte = np.maximum(np.where(amax > 0, np.frexp(amax)[1] - 1 + 127, 0) - down, 1)
    scale = np.exp2(byte - 127.0)
    codes = (blocks / scale).astype(np.float32).astype(dtype).astype(np.float64)
    return np.moveaxis((codes * scale).reshape(v.shape), -1, axis)


WIDE = False


def mx_kscale(k):
    if not WIDE:
        return np.ones(k)
    levels = np.array([10, -10, 5, -5, 0])
    if k % 512:
        return np.exp2(np.random.permutation(np.resize(levels, k // 32))).repeat(32)
    a = np.empty((k // 512, 16))
    for p in range(k // 512):
        a[p, :8] = np.random.permutation(np.resize(levels, 8))
        for g in range(8):
            far = levels[np.abs(levels - a[p, g]) >= 10]
            a[p, g + 8] = far[np.random.randint(len(far))]
    return np.exp2(a.ravel()).repeat(32)


def f64(x):
    return np.asarray(x).astype(np.float64)


def striped(idx):
    return np.tile(idx.reshape(-1, 16).T, (8, 1)).astype(np.uint16)


def unstriped(offs):
    return offs[:16].T.reshape(-1).astype(np.int64)


E2M1 = np.array([0.0, 0.5, 1.0, 1.5, 2.0, 3.0, 4.0, 6.0, -0.0, -0.5, -1.0, -1.5, -2.0, -3.0, -4.0, -6.0])


def pack_weight(w, fmt):
    k, n = w.shape
    w = f64(np.asarray(w, np.float32).astype(ml_dtypes.bfloat16)).reshape(k // 32, 32, n)
    amax = np.abs(w).max(1)
    if fmt == "e4m3":
        byte = np.frexp(amax)[1] - 1 + 127 - 7
    else:
        mant, ex = np.frexp(amax / 6.0)
        byte = np.where(mant > 0.5, ex, ex - 1) + 127
    byte = np.clip(np.where(amax > 0, byte, 1), 1, 254)
    scaled = (w * np.exp2(127.0 - byte)[:, None, :]).reshape(k, n).astype(np.float32)
    by_word = np.ascontiguousarray(scaled.reshape(k // 512, 128, 4, n).transpose(0, 1, 3, 2))
    if fmt == "e4m3":
        words = by_word.astype(ml_dtypes.float8_e4m3fn).view(np.uint8)
    else:
        c = by_word.astype(ml_dtypes.float4_e2m1fn).view(np.uint8) & 0xF
        words = (c[..., 0::2] | (c[..., 1::2] << 4)).reshape(k // 512, 128, 2 * n)
    return np.ascontiguousarray(words), np.ascontiguousarray(byte.astype(np.uint8).reshape(k // 512, 16, n))


def unpack_weight(words, scales, fmt):
    g, _, n = scales.shape
    words = np.ascontiguousarray(words).reshape(g, 128, n, -1)
    if fmt == "e4m3":
        vals = words.view(ml_dtypes.float8_e4m3fn).astype(np.float64)
    else:
        nib = np.empty((g, 128, n, 4), np.uint8)
        nib[..., 0::2] = words & 0xF
        nib[..., 1::2] = words >> 4
        vals = E2M1[nib]
    vals = vals * np.repeat(np.exp2(scales.astype(np.float64) - 127.0), 8, axis=1)[..., None]
    return vals.transpose(0, 1, 3, 2).reshape(g * 512, n)


def gelu(v):
    return 0.5 * v * (1.0 + np.tanh(np.sqrt(2.0 / np.pi) * (v + 0.044715 * v**3)))


def bf(x):
    return np.asarray(x, np.float32).astype(ml_dtypes.bfloat16)


def planes(Y):
    n, m = Y.shape
    b = f64(bf(Y)).reshape(n // 32, 32, m)
    amax = np.abs(b).max(1)
    byte = np.clip(np.where(amax > 0, np.frexp(amax)[1] - 1 + 127 - 7, 1), 1, 254)
    codes = (b * np.exp2(127.0 - byte)[:, None, :]).reshape(n, m).astype(np.float32).astype(ml_dtypes.float8_e4m3fn).view(np.uint8)
    words = codes.reshape(n // 512, 128, 4, m).transpose(0, 1, 3, 2)
    return np.ascontiguousarray(words), np.ascontiguousarray(byte.astype(np.uint8).reshape(n // 512, 16, m))


K, H, N, T, S, P = 512, 1536, 512, 4096, 1024, 512

def setup_inputs():
    n = np.random.standard_normal
    s = mx_kscale(K)[:, None]
    u = mx_kscale(H)[:, None]
    d = {}
    d["tab_words"], d["tab_scales"] = pack_weight(n((K, T)) * s, "e4m3")
    d["offs"] = striped(np.random.permutation(T)[:S])
    d["pos1"] = striped(np.random.permutation(S)[:P])
    d["pos2"] = striped(np.random.permutation(S)[:P])
    d["w1"] = (n((K, H)) / K**0.5 / s).astype(np.float32)
    d["w4_words"], d["w4_scales"] = pack_weight(1.2 * n((K, H)) / K**0.5 / s, "e2m1")
    d["gain"] = (np.exp(0.3 * n(H)) * u[:, 0]).astype(np.float32)
    d["w3"] = (0.7 * n((H, N)) / H**0.5 / u * np.exp(0.8 * n(N))[None, :]).astype(np.float32)
    d["beside"] = (0.8 * n(N)).astype(np.float32)
    return d

def reference(tab_words, tab_scales, offs, pos1, pos2, w1, w4_words, w4_scales, gain, w3, beside):
    v = unpack_weight(tab_words, tab_scales, "e4m3")[:, unstriped(offs)]
    w4 = unpack_weight(w4_words, w4_scales, "e2m1")
    stripe = mxq(f64(w1), 0, "e4m3").T @ v
    level = w4.T @ v
    h = np.abs(np.abs(stripe) - level) * f64(gain)[:, None]
    t3 = mxq(f64(w3), 0, "e4m3").T @ mxq(h, 0, "e4m3")
    g2 = t3 / (1.0 + np.exp(-t3))
    y = g2[:, unstriped(pos1)] + f64(beside)[:, None] * g2[:, unstriped(pos2)]
    words, scales = planes(y)
    return y, words, scales

@@ -1,0 +1,292 @@
+from contextlib import ExitStack
+
+import concourse.mybir as mybir
+
+K, H, N, T, S, M = 512, 1536, 512, 4096, 1024, 512
+FLOPS = 2 * (2 * K * H * S + H * N * S)
+
+F32 = mybir.dt.float32
+BF16 = mybir.dt.bfloat16
+I32 = mybir.dt.int32
+U32 = mybir.dt.uint32
+U16 = mybir.dt.uint16
+U8 = mybir.dt.uint8
+FP8X4 = mybir.dt.float8_e4m3fn_x4
+FP4X4 = mybir.dt.float4_e2m1fn_x4
+ALU = mybir.AluOpType
+ACT = mybir.ActivationFunctionType
+
+P = 128
+PACK = 4
+PASS = P * PACK
+PASSES = H // PASS
+HALF = 512
+HALVES = S // HALF
+LIST_ROWS = 16
+
+
+def tile_list_plank_pair_features_kernel(
+    tc, tab_words, tab_scales, offs, pos1, pos2, w1, w4_words, w4_scales, gain, w3, beside, out_0, out_1, out_2
+):
+    nc = tc.nc
+    with ExitStack() as ctx:
+        lists = ctx.enter_context(tc.tile_pool(name="lists", bufs=1))
+        keep = ctx.enter_context(tc.tile_pool(name="keep", bufs=1))
+        work = ctx.enter_context(tc.tile_pool(name="work", bufs=2))
+        psum = ctx.enter_context(tc.psum_pool(name="psum", bufs=1))
+
+        offs_sb = lists.tile([P, S // LIST_ROWS], U16, name="offs_sb")
+        pos1_sb = lists.tile([P, M // LIST_ROWS], U16, name="pos1_sb")
+        pos2_sb = lists.tile([P, M // LIST_ROWS], U16, name="pos2_sb")
+
+        table = keep.tile([P, T], I32, name="table")
+        table_scales = keep.tile([P, T], U8, name="table_scales")
+        w4_raw = keep.tile([P, 2 * H], U8, name="w4_raw")
+        w4_raw_scales = keep.tile([P, H], U8, name="w4_raw_scales")
+        gain_sb = keep.tile([P, PASSES, PACK], F32, name="gain_sb")
+        beside_sb = keep.tile([P, PACK], F32, name="beside_sb")
+        w1_raw, w3_raw = {}, {}
+
+        warm = keep.tile([P, 2], F32, name="warm")
+        nc.gpsimd.memset(w4_raw_scales[:].bitcast(I32), 0)
+        nc.vector.memset(table_scales[:].bitcast(I32), 0)
+        nc.vector.memset(warm[:, 0:1], 0.0)
+
+        def load_scale_rows(queue, tile, rows):
+            for r in range(4):
+                queue.dma_start(out=tile[r:P:32, :].bitcast(I32), in_=rows[r:16:4, :].bitcast(I32))
+
+        def load_w1(b):
+            cols = w1[:, b * PASS : (b + 1) * PASS]
+            w1_raw[b] = work.tile([P, PACK, PASS], F32, name="raw", bufs=3)
+            nc.sync.dma_start(out=w1_raw[b][:], in_=cols.rearrange("(p j) c -> p j c", j=PACK))
+
+        def load_w3(b):
+            rows = w3[b * PASS : (b + 1) * PASS, :]
+            w3_raw[b] = work.tile([P, PACK, N], F32, name="raw", bufs=3)
+            nc.sync.dma_start(out=w3_raw[b][:], in_=rows.rearrange("(p j) n -> p j n", j=PACK))
+
+        nc.scalar.activation(warm[:, 1:2], warm[:, 0:1], ACT.Silu)
+        nc.sync.dma_start(offs_sb[:], offs)
+        nc.sync.dma_start(out=gain_sb[:], in_=gain.rearrange("(b p t) -> p b t", p=P, t=PACK))
+        load_w1(0)
+        load_scale_rows(nc.sync, table_scales, tab_scales[0])
+        nc.sync.dma_start(out=w4_raw[:].bitcast(I32), in_=w4_words[0].bitcast(I32))
+        nc.sync.dma_start(out=table[:], in_=tab_words[0].rearrange("p n t -> p (n t)").bitcast(I32))
+        load_scale_rows(nc.sync, w4_raw_scales, w4_scales[0])
+        load_w1(1)
+        load_w1(2)
+        nc.sync.dma_start(pos1_sb[:], pos1)
+        nc.sync.dma_start(pos2_sb[:], pos2)
+        nc.sync.dma_start(out=beside_sb[:], in_=beside.rearrange("(p t) -> p t", t=PACK))
+
+        picked_scales = keep.tile([P, S], U8, name="picked_scales", align_bytes=64)
+        picked = [keep.tile([P, HALF], U32, name="picked%d" % h, align_bytes=64) for h in range(HALVES)]
+
+        def gather_words(h):
+            cols = HALF // LIST_ROWS
+            nc.vector.tensor_copy(picked[h][:], table[:].bitcast(U32).indirect(offs_sb[:, h * cols : (h + 1) * cols]))
+
+        w4_codes, w4_planes, w1_codes, w1_planes, w3_codes, w3_planes = {}, {}, {}, {}, {}, {}
+
+        def deal_w4(b):
+            codes = keep.tile([P, 2 * PASS], U8, name="w4_codes%d" % b, align_bytes=64)
+            plane = keep.tile([P, PASS], U8, name="w4_plane%d" % b, align_bytes=64)
+            nc.vector.tensor_copy(
+                out=codes[:].rearrange("p (t m x) -> p t m x", t=PACK, x=2),
+                in_=w4_raw[:, 2 * b * PASS : 2 * (b + 1) * PASS].rearrange("p (m t x) -> p t m x", t=PACK, x=2),
+            )
+            nc.vector.tensor_copy(
+                out=plane[:].rearrange("p (t m) -> p t m", t=PACK),
+                in_=w4_raw_scales[:, b * PASS : (b + 1) * PASS].rearrange("p (m t) -> p t m", t=PACK),
+            )
+            w4_codes[b], w4_planes[b] = codes, plane
+
+        def dealt_views(rounded, raw, u):
+            src = raw[:].rearrange("p j (m u e) -> p u m j e", u=2, e=2)[:, u]
+            dst = rounded[:].rearrange("p (e m j) -> p m j e", e=2, j=PACK)
+            return dst, src
+
+        def quantize(rounded, name):
+            words = rounded.shape[1] // PACK
+            codes = keep.tile([P, words], U32, name=name + "_codes", align_bytes=64)
+            plane = keep.tile([P, words], U8, name=name + "_plane", align_bytes=64)
+            nc.vector.quantize_mx(out=codes[:].bitcast(FP8X4), scales=plane[:], in_=rounded[:])
+            return codes, plane
+
+        def round_w1(b, u, on_scalar):
+            rounded = work.tile([P, 2 * P * PACK], BF16, name="w_rounded", bufs=4, align_bytes=64)
+            dst, src = dealt_views(rounded, w1_raw[b], u)
+            if on_scalar:
+                nc.scalar.copy(out=dst, in_=src)
+            else:
+                nc.vector.tensor_copy(out=dst, in_=src)
+            return rounded
+
+        def round_w3(b, u):
+            rounded = work.tile([P, 2 * P * PACK], BF16, name="w_rounded", bufs=4, align_bytes=64)
+            dst, src = dealt_views(rounded, w3_raw[b], u)
+            signs = sign[:, b].unsqueeze(1).to_broadcast([P, P, PACK, 2])
+            nc.vector.tensor_tensor(out=dst, in0=src, in1=signs, op=ALU.mult)
+            return rounded
+
+        def prep_w1(b, on_scalar):
+            rounded = [round_w1(b, u, on_scalar) for u in range(2)]
+            for u in range(2):
+                w1_codes[b, u], w1_planes[b, u] = quantize(rounded[u], "w1_%d_%d" % (b, u))
+
+        w3_rounded = {}
+
+        def start_w3(b, u):
+            w3_rounded[b, u] = round_w3(b, u)
+
+        def end_w3(b, u):
+            w3_codes[b, u], w3_planes[b, u] = quantize(w3_rounded[b, u], "w3_%d_%d" % (b, u))
+
+        nc.vector.tensor_copy(picked_scales[:], table_scales[:].indirect(offs_sb[:]))
+        prep_w1(0, True)
+        load_w3(0)
+        gather_words(0)
+        for b in range(PASSES):
+            deal_w4(b)
+
+        sign01 = keep.tile([P, PASSES, PACK, 2], F32, name="sign01")
+        sign = keep.tile([P, PASSES, PACK, 2], F32, name="sign")
+        gain_size = keep.tile([P, PASSES, PACK], F32, name="gain_size")
+        nc.vector.tensor_scalar(
+            out=sign01[:], in0=gain_sb[:].unsqueeze(3).to_broadcast([P, PASSES, PACK, 2]),
+            scalar1=0.0, scalar2=2.0, op0=ALU.is_ge, op1=ALU.mult,
+        )
+        nc.vector.tensor_scalar(out=sign[:], in0=sign01[:], scalar1=-1.0, scalar2=None, op0=ALU.add)
+        nc.vector.tensor_tensor(out=gain_size[:], in0=gain_sb[:], in1=sign[:, :, :, 0], op=ALU.mult)
+
+        h_codes, h_planes, diffs = {}, {}, {}
+        g2 = [keep.tile([P, S], F32, name="g2_%d" % t) for t in range(PACK)]
+
+        def first_stage(h, b, t):
+            u, e = divmod(t, 2)
+            cols = slice(e * P, (e + 1) * P)
+            moving = picked[h][:].bitcast(FP8X4)
+            moving_plane = picked_scales[:, h * HALF : (h + 1) * HALF]
+            stripe = psum.tile([P, HALF], F32, name="stripe", bufs=3)
+            level = psum.tile([P, HALF], F32, name="level", bufs=3)
+            nc.tensor.matmul_mx(
+                out=stripe[:], lhsT=w1_codes[b, u][:, cols].bitcast(FP8X4), lhsT_scale=w1_planes[b, u][:, cols],
+                rhs=moving, rhs_scale=moving_plane, start=True, stop=True,
+            )
+            nc.tensor.matmul_mx(
+                out=level[:], lhsT=w4_codes[b][:, 2 * t * P : 2 * (t + 1) * P].bitcast(FP4X4),
+                lhsT_scale=w4_planes[b][:, t * P : (t + 1) * P],
+                rhs=moving, rhs_scale=moving_plane, start=True, stop=True,
+            )
+            size = work.tile([P, HALF], F32, name="size", bufs=4)
+            nc.scalar.activation(size[:], stripe[:], ACT.Abs, scale=gain_sb[:, b, t : t + 1])
+            if t == 0:
+                diffs[h, b] = work.tile([P, PACK, HALF], BF16, name="diff", bufs=3)
+            nc.vector.scalar_tensor_tensor(
+                out=diffs[h, b][:, t, :], in0=level[:], scalar=gain_size[:, b, t : t + 1], in1=size[:],
+                op0=ALU.mult, op1=ALU.subtract,
+            )
+
+        def finish_h(h, b, c):
+            width = HALF // 2
+            cols = slice(c * width, (c + 1) * width)
+            if c == 0:
+                h_codes[h, b] = keep.tile([P, HALF], U32, name="h_codes%d_%d" % (h, b), align_bytes=64)
+                h_planes[h, b] = keep.tile([P, HALF], U8, name="h_plane%d_%d" % (h, b), align_bytes=64)
+            woven = work.tile([P, width * PACK], BF16, name="woven", bufs=3, align_bytes=64)
+            nc.scalar.activation(
+                woven[:].rearrange("p (c i t) -> p c t i", i=4, t=PACK),
+                diffs[h, b][:, :, cols].rearrange("p t (c i) -> p c t i", i=4),
+                ACT.Abs,
+            )
+            nc.vector.quantize_mx(out=h_codes[h, b][:, cols].bitcast(FP8X4), scales=h_planes[h, b][:, cols], in_=woven[:])
+
+        def second_stage(h, t):
+            u, e = divmod(t, 2)
+            cols = slice(e * P, (e + 1) * P)
+            acc = psum.tile([P, HALF], F32, name="acc", bufs=2)
+            for b in range(PASSES):
+                nc.tensor.matmul_mx(
+                    out=acc[:], lhsT=w3_codes[b, u][:, cols].bitcast(FP8X4), lhsT_scale=w3_planes[b, u][:, cols],
+                    rhs=h_codes[h, b][:].bitcast(FP8X4), rhs_scale=h_planes[h, b][:],
+                    start=(b == 0), stop=(b == PASSES - 1),
+                )
+            nc.scalar.activation(g2[t][:, h * HALF : (h + 1) * HALF], acc[:], ACT.Silu)
+
+        between = {
+            (0, 1): [lambda: prep_w1(1, True), lambda: load_w3(1)],
+            (0, 3): [lambda: gather_words(1)],
+            (1, 1): [lambda: prep_w1(2, False), lambda: load_w3(2)],
+            (2, 2): [lambda: start_w3(0, 0)],
+            (2, 3): [lambda: end_w3(0, 0)],
+            (3, 2): [lambda: start_w3(1, 0)],
+            (3, 3): [lambda: end_w3(1, 0)],
+            (4, 2): [lambda: start_w3(2, 0)],
+            (4, 3): [lambda: end_w3(2, 0)],
+            (5, 1): [lambda: second_stage(0, 0)],
+            (5, 2): [lambda: start_w3(0, 1)],
+            (5, 3): [lambda: end_w3(0, 1)],
+        }
+        groups = [(h, b) for h in range(HALVES) for b in range(PASSES)]
+        for g, (h, b) in enumerate(groups):
+            for t in range(PACK):
+                first_stage(h, b, t)
+                if g > 0 and t < 2:
+                    finish_h(*groups[g - 1], t)
+                for job in between.get((g, t), []):
+                    job()
+        for c in range(2):
+            finish_h(*groups[-1], c)
+        second_stage(1, 0)
+        for b in (1, 2):
+            start_w3(b, 1)
+        for b in (1, 2):
+            end_w3(b, 1)
+        for t in range(1, PACK):
+            for h in range(HALVES):
+                second_stage(h, t)
+
+        y = keep.tile([P, PACK, M], F32, name="y")
+        y_codes = keep.tile([P, M], U32, name="y_codes", align_bytes=64)
+        y_plane = keep.tile([P, M], U8, name="y_plane", align_bytes=64)
+        out_rows = out_0.rearrange("(p t) m -> p t m", t=PACK)
+        out_words = out_1[0].rearrange("p m t -> p (m t)").bitcast(I32)
+
+        def pick_beside(t, c0, c1):
+            other = work.tile([P, c1 - c0], F32, name="other", bufs=3)
+            weighted = work.tile([P, c1 - c0], F32, name="weighted", bufs=3)
+            nc.vector.tensor_copy(other[:], g2[t][:].indirect(pos2_sb[:, c0 // LIST_ROWS : c1 // LIST_ROWS]))
+            nc.scalar.activation(weighted[:], other[:], ACT.Copy, scale=beside_sb[:, t : t + 1])
+            return weighted
+
+        def pick_own(t, c0, c1, weighted):
+            nc.vector.tensor_tensor(
+                y[:, t, c0:c1], g2[t][:].indirect(pos1_sb[:, c0 // LIST_ROWS : c1 // LIST_ROWS]), weighted[:], ALU.add
+            )
+            nc.sync.dma_start(out=out_rows[:, t, c0:c1], in_=y[:, t, c0:c1])
+
+        def planes_of(c0, c1, on_scalar):
+            woven = work.tile([P, (c1 - c0) * PACK], BF16, name="y_woven", bufs=2, align_bytes=64)
+            dst = woven[:].rearrange("p (c i t) -> p c t i", i=4, t=PACK)
+            src = y[:, :, c0:c1].rearrange("p t (c i) -> p c t i", i=4)
+            if on_scalar:
+                nc.scalar.copy(out=dst, in_=src)
+            else:
+                nc.vector.tensor_copy(out=dst, in_=src)
+            nc.vector.quantize_mx(out=y_codes[:, c0:c1].bitcast(FP8X4), scales=y_plane[:, c0:c1], in_=woven[:])
+            nc.scalar.dma_start(out=out_words[:, c0:c1], in_=y_codes[:, c0:c1].bitcast(I32))
+
+        pieces = [(0, 0, M), (1, 0, M), (2, 0, M), (3, 0, M // 2), (3, M // 2, M)]
+        weighted = pick_beside(*pieces[0])
+        for i, piece in enumerate(pieces):
+            ahead = pick_beside(*pieces[i + 1]) if i + 1 < len(pieces) else None
+            pick_own(*piece, weighted)
+            weighted = ahead
+        planes_of(0, M // 2, True)
+        planes_of(M // 2, M, False)
+        for q in range(4):
+            queue = nc.sync if q % 2 == 0 else nc.scalar
+            queue.dma_start(
+                out=out_2[0, 4 * q : 4 * q + 4, :].bitcast(I32), in_=y_plane[32 * q : 32 * q + 4, :].bitcast(I32)
+            )

@@ -20,9 +20,13 @@ P = 128
 PACK = 4
 PASS = P * PACK
 PASSES = H // PASS
-HALF = 512
-HALVES = S // HALF
-LIST_ROWS = 16
+BANK = 512
+HALVES = S // BANK
+BLOCKS = PASS // 32
+QUADRANT = 32
+STRIPE = 16
+PIECE = 256
+NEIGHBOURS = 4
 
 
 def tile_list_plank_pair_features_kernel(
@@ -32,218 +36,221 @@ def tile_list_plank_pair_features_kernel(
     with ExitStack() as ctx:
         lists = ctx.enter_context(tc.tile_pool(name="lists", bufs=1))
         keep = ctx.enter_context(tc.tile_pool(name="keep", bufs=1))
-        work = ctx.enter_context(tc.tile_pool(name="work", bufs=2))
-        psum = ctx.enter_context(tc.psum_pool(name="psum", bufs=1))
+        work = ctx.enter_context(tc.tile_pool(name="work", bufs=3))
+        psum = ctx.enter_context(tc.psum_pool(name="psum", bufs=3))
 
-        offs_sb = lists.tile([P, S // LIST_ROWS], U16, name="offs_sb")
-        pos1_sb = lists.tile([P, M // LIST_ROWS], U16, name="pos1_sb")
-        pos2_sb = lists.tile([P, M // LIST_ROWS], U16, name="pos2_sb")
+        w1_tags = ("w1_first", "a", "b")
+        w3_tags = ("c", "a", "b")
 
-        table = keep.tile([P, T], I32, name="table")
+        offs_sb = lists.tile([P, S // STRIPE], U16, name="offs_sb")
+        pos1_sb = lists.tile([P, M // STRIPE], U16, name="pos1_sb")
+        pos2_sb = lists.tile([P, M // STRIPE], U16, name="pos2_sb")
+        table = keep.tile([P, T], I32, name="table", tag="c")
         table_scales = keep.tile([P, T], U8, name="table_scales")
         w4_raw = keep.tile([P, 2 * H], U8, name="w4_raw")
         w4_raw_scales = keep.tile([P, H], U8, name="w4_raw_scales")
         gain_sb = keep.tile([P, PASSES, PACK], F32, name="gain_sb")
         beside_sb = keep.tile([P, PACK], F32, name="beside_sb")
+        planes = keep.tile([P, S + H], U8, name="planes", align_bytes=64)
         w1_raw, w3_raw = {}, {}
 
-        warm = keep.tile([P, 2], F32, name="warm")
         nc.gpsimd.memset(w4_raw_scales[:].bitcast(I32), 0)
         nc.vector.memset(table_scales[:].bitcast(I32), 0)
-        nc.vector.memset(warm[:, 0:1], 0.0)
+        nc.vector.memset(planes[:].bitcast(I32), 0)
 
-        def load_scale_rows(queue, tile, rows):
-            for r in range(4):
-                queue.dma_start(out=tile[r:P:32, :].bitcast(I32), in_=rows[r:16:4, :].bitcast(I32))
+        warm = keep.tile([P, 2], F32, name="warm")
+        nc.vector.memset(warm[:, 0:1], 0.0)
+        nc.scalar.activation(warm[:, 1:2], warm[:, 0:1], ACT.Silu)
 
         def load_w1(b):
-            cols = w1[:, b * PASS : (b + 1) * PASS]
-            w1_raw[b] = work.tile([P, PACK, PASS], F32, name="raw", bufs=3)
-            nc.sync.dma_start(out=w1_raw[b][:], in_=cols.rearrange("(p j) c -> p j c", j=PACK))
+            w1_raw[b] = keep.tile([P, PACK, PASS], F32, name="w1_raw%d" % b, tag=w1_tags[b])
+            columns = w1[:, b * PASS : (b + 1) * PASS]
+            nc.sync.dma_start(out=w1_raw[b][:], in_=columns.rearrange("(p j) c -> p j c", j=PACK))
 
         def load_w3(b):
+            w3_raw[b] = keep.tile([P, PACK, N], F32, name="w3_raw%d" % b, tag=w3_tags[b])
             rows = w3[b * PASS : (b + 1) * PASS, :]
-            w3_raw[b] = work.tile([P, PACK, N], F32, name="raw", bufs=3)
             nc.sync.dma_start(out=w3_raw[b][:], in_=rows.rearrange("(p j) n -> p j n", j=PACK))
 
-        nc.scalar.activation(warm[:, 1:2], warm[:, 0:1], ACT.Silu)
         nc.sync.dma_start(offs_sb[:], offs)
+        nc.sync.dma_start(out=w4_raw_scales[0:BLOCKS, :].bitcast(I32), in_=w4_scales[0].bitcast(I32))
+        nc.sync.dma_start(out=table_scales[0:BLOCKS, :].bitcast(I32), in_=tab_scales[0].bitcast(I32))
         nc.sync.dma_start(out=gain_sb[:], in_=gain.rearrange("(b p t) -> p b t", p=P, t=PACK))
-        load_w1(0)
-        load_scale_rows(nc.sync, table_scales, tab_scales[0])
-        nc.sync.dma_start(out=w4_raw[:].bitcast(I32), in_=w4_words[0].bitcast(I32))
         nc.sync.dma_start(out=table[:], in_=tab_words[0].rearrange("p n t -> p (n t)").bitcast(I32))
-        load_scale_rows(nc.sync, w4_raw_scales, w4_scales[0])
-        load_w1(1)
-        load_w1(2)
-        nc.sync.dma_start(pos1_sb[:], pos1)
-        nc.sync.dma_start(pos2_sb[:], pos2)
         nc.sync.dma_start(out=beside_sb[:], in_=beside.rearrange("(p t) -> p t", t=PACK))
+        nc.sync.dma_start(pos1_sb[:], pos1)
+        load_w1(0)
+        nc.sync.dma_start(out=w4_raw[:].bitcast(I32), in_=w4_words[0].bitcast(I32))
+        nc.sync.dma_start(pos2_sb[:], pos2)
 
-        picked_scales = keep.tile([P, S], U8, name="picked_scales", align_bytes=64)
-        picked = [keep.tile([P, HALF], U32, name="picked%d" % h, align_bytes=64) for h in range(HALVES)]
-
-        def gather_words(h):
-            cols = HALF // LIST_ROWS
-            nc.vector.tensor_copy(picked[h][:], table[:].bitcast(U32).indirect(offs_sb[:, h * cols : (h + 1) * cols]))
-
-        w4_codes, w4_planes, w1_codes, w1_planes, w3_codes, w3_planes = {}, {}, {}, {}, {}, {}
-
-        def deal_w4(b):
-            codes = keep.tile([P, 2 * PASS], U8, name="w4_codes%d" % b, align_bytes=64)
-            plane = keep.tile([P, PASS], U8, name="w4_plane%d" % b, align_bytes=64)
+        picked_scales = keep.tile([P, S], U8, name="picked_scales", tag="a")
+        staged = keep.tile([P, S + H], U8, name="staged", tag="b")
+        for b in range(PASSES):
             nc.vector.tensor_copy(
-                out=codes[:].rearrange("p (t m x) -> p t m x", t=PACK, x=2),
-                in_=w4_raw[:, 2 * b * PASS : 2 * (b + 1) * PASS].rearrange("p (m t x) -> p t m x", t=PACK, x=2),
-            )
-            nc.vector.tensor_copy(
-                out=plane[:].rearrange("p (t m) -> p t m", t=PACK),
+                out=staged[:, S + b * PASS : S + (b + 1) * PASS].rearrange("p (t m) -> p t m", t=PACK),
                 in_=w4_raw_scales[:, b * PASS : (b + 1) * PASS].rearrange("p (m t) -> p t m", t=PACK),
             )
-            w4_codes[b], w4_planes[b] = codes, plane
+        nc.vector.tensor_copy(picked_scales[:], table_scales[:].indirect(offs_sb[:]))
+        nc.vector.tensor_copy(out=staged[:, 0:S].bitcast(I32), in_=picked_scales[:].bitcast(I32))
+        for q in range(P // QUADRANT):
+            nc.sync.dma_start(
+                out=planes[QUADRANT * q : QUADRANT * q + 4, :].bitcast(I32), in_=staged[4 * q : 4 * q + 4, :].bitcast(I32)
+            )
+        load_w1(1)
+        load_w1(2)
 
-        def dealt_views(rounded, raw, u):
+        picked = [keep.tile([P, BANK], U32, name="picked%d" % h, align_bytes=64) for h in range(HALVES)]
+        w4_codes, w1_mx, w3_mx, w3_woven = {}, {}, {}, {}
+
+        def gather_words(h):
+            entries = offs_sb[:, h * BANK // STRIPE : (h + 1) * BANK // STRIPE]
+            nc.vector.tensor_copy(picked[h][:], table[:].bitcast(U32).indirect(entries))
+
+        def deal_w4(b):
+            w4_codes[b] = keep.tile([P, 2 * PASS], U8, name="w4_codes%d" % b, align_bytes=64)
+            nc.vector.tensor_copy(
+                out=w4_codes[b][:].bitcast(U16).rearrange("p (t m) -> p t m", t=PACK),
+                in_=w4_raw[:].bitcast(U16)[:, b * PASS : (b + 1) * PASS].rearrange("p (m t) -> p t m", t=PACK),
+            )
+
+        def dealt_views(woven, raw, u):
             src = raw[:].rearrange("p j (m u e) -> p u m j e", u=2, e=2)[:, u]
-            dst = rounded[:].rearrange("p (e m j) -> p m j e", e=2, j=PACK)
+            dst = woven[:].rearrange("p (e m j) -> p m j e", e=2, j=PACK)
             return dst, src
 
-        def quantize(rounded, name):
-            words = rounded.shape[1] // PACK
-            codes = keep.tile([P, words], U32, name=name + "_codes", align_bytes=64)
-            plane = keep.tile([P, words], U8, name=name + "_plane", align_bytes=64)
-            nc.vector.quantize_mx(out=codes[:].bitcast(FP8X4), scales=plane[:], in_=rounded[:])
+        def quantize_weight(woven, name):
+            codes = keep.tile([P, 2 * P], U32, name=name + "_codes", align_bytes=64)
+            plane = keep.tile([P, 2 * P], U8, name=name + "_plane", align_bytes=64)
+            nc.vector.quantize_mx(out=codes[:].bitcast(FP8X4), scales=plane[:], in_=woven[:])
             return codes, plane
 
-        def round_w1(b, u, on_scalar):
-            rounded = work.tile([P, 2 * P * PACK], BF16, name="w_rounded", bufs=4, align_bytes=64)
-            dst, src = dealt_views(rounded, w1_raw[b], u)
-            if on_scalar:
-                nc.scalar.copy(out=dst, in_=src)
-            else:
-                nc.vector.tensor_copy(out=dst, in_=src)
-            return rounded
-
-        def round_w3(b, u):
-            rounded = work.tile([P, 2 * P * PACK], BF16, name="w_rounded", bufs=4, align_bytes=64)
-            dst, src = dealt_views(rounded, w3_raw[b], u)
-            signs = sign[:, b].unsqueeze(1).to_broadcast([P, P, PACK, 2])
-            nc.vector.tensor_tensor(out=dst, in0=src, in1=signs, op=ALU.mult)
-            return rounded
-
-        def prep_w1(b, on_scalar):
-            rounded = [round_w1(b, u, on_scalar) for u in range(2)]
+        def prepare_w1(b, copies):
+            woven = [work.tile([P, 2 * PASS], BF16, name="w1_woven", bufs=4, align_bytes=64) for u in range(2)]
             for u in range(2):
-                w1_codes[b, u], w1_planes[b, u] = quantize(rounded[u], "w1_%d_%d" % (b, u))
+                dst, src = dealt_views(woven[u], w1_raw[b], u)
+                copies[u](out=dst, in_=src)
+            for u in range(2):
+                w1_mx[b, u] = quantize_weight(woven[u], "w1_%d_%d" % (b, u))
 
-        w3_rounded = {}
+        def weave_w3(b, u, woven):
+            dst, src = dealt_views(woven, w3_raw[b], u)
+            signs = sign[:, b].unsqueeze(1).unsqueeze(3).to_broadcast([P, P, PACK, 2])
+            nc.vector.tensor_tensor(out=dst, in0=src, in1=signs, op=ALU.mult)
+            w3_woven[b, u] = woven
 
-        def start_w3(b, u):
-            w3_rounded[b, u] = round_w3(b, u)
+        def quantize_w3(b, u):
+            w3_mx[b, u] = quantize_weight(w3_woven[b, u], "w3_%d_%d" % (b, u))
 
-        def end_w3(b, u):
-            w3_codes[b, u], w3_planes[b, u] = quantize(w3_rounded[b, u], "w3_%d_%d" % (b, u))
-
-        nc.vector.tensor_copy(picked_scales[:], table_scales[:].indirect(offs_sb[:]))
-        prep_w1(0, True)
-        load_w3(0)
+        on_vector, on_scalar = nc.vector.tensor_copy, nc.scalar.copy
         gather_words(0)
+        prepare_w1(0, (on_vector, on_scalar))
         for b in range(PASSES):
             deal_w4(b)
+        gather_words(1)
 
-        sign01 = keep.tile([P, PASSES, PACK, 2], F32, name="sign01")
-        sign = keep.tile([P, PASSES, PACK, 2], F32, name="sign")
+        sign_plus_one = keep.tile([P, PASSES, PACK], F32, name="sign_plus_one")
+        sign = keep.tile([P, PASSES, PACK], F32, name="sign")
         gain_size = keep.tile([P, PASSES, PACK], F32, name="gain_size")
         nc.vector.tensor_scalar(
-            out=sign01[:], in0=gain_sb[:].unsqueeze(3).to_broadcast([P, PASSES, PACK, 2]),
-            scalar1=0.0, scalar2=2.0, op0=ALU.is_ge, op1=ALU.mult,
+            out=sign_plus_one[:], in0=gain_sb[:], scalar1=0.0, scalar2=2.0, op0=ALU.is_ge, op1=ALU.mult
         )
-        nc.vector.tensor_scalar(out=sign[:], in0=sign01[:], scalar1=-1.0, scalar2=None, op0=ALU.add)
-        nc.vector.tensor_tensor(out=gain_size[:], in0=gain_sb[:], in1=sign[:, :, :, 0], op=ALU.mult)
+        nc.vector.tensor_scalar(out=sign[:], in0=sign_plus_one[:], scalar1=-1.0, scalar2=None, op0=ALU.add)
+        nc.scalar.activation(gain_size[:], gain_sb[:], ACT.Abs)
 
         h_codes, h_planes, diffs = {}, {}, {}
         g2 = [keep.tile([P, S], F32, name="g2_%d" % t) for t in range(PACK)]
 
-        def first_stage(h, b, t):
+        def first_stage(h, b, t, size):
             u, e = divmod(t, 2)
-            cols = slice(e * P, (e + 1) * P)
+            codes, plane = w1_mx[b, u]
             moving = picked[h][:].bitcast(FP8X4)
-            moving_plane = picked_scales[:, h * HALF : (h + 1) * HALF]
-            stripe = psum.tile([P, HALF], F32, name="stripe", bufs=3)
-            level = psum.tile([P, HALF], F32, name="level", bufs=3)
+            moving_plane = planes[:, h * BANK : (h + 1) * BANK]
+            w4_column = S + b * PASS + t * P
+            stripe = psum.tile([P, BANK], F32, name="stripe")
+            level = psum.tile([P, BANK], F32, name="level")
             nc.tensor.matmul_mx(
-                out=stripe[:], lhsT=w1_codes[b, u][:, cols].bitcast(FP8X4), lhsT_scale=w1_planes[b, u][:, cols],
+                out=stripe[:], lhsT=codes[:, e * P : (e + 1) * P].bitcast(FP8X4), lhsT_scale=plane[:, e * P : (e + 1) * P],
                 rhs=moving, rhs_scale=moving_plane, start=True, stop=True,
             )
             nc.tensor.matmul_mx(
                 out=level[:], lhsT=w4_codes[b][:, 2 * t * P : 2 * (t + 1) * P].bitcast(FP4X4),
-                lhsT_scale=w4_planes[b][:, t * P : (t + 1) * P],
+                lhsT_scale=planes[:, w4_column : w4_column + P],
                 rhs=moving, rhs_scale=moving_plane, start=True, stop=True,
             )
-            size = work.tile([P, HALF], F32, name="size", bufs=4)
             nc.scalar.activation(size[:], stripe[:], ACT.Abs, scale=gain_sb[:, b, t : t + 1])
             if t == 0:
-                diffs[h, b] = work.tile([P, PACK, HALF], BF16, name="diff", bufs=3)
+                diffs[h, b] = work.tile([P, PACK, BANK], BF16, name="diff")
             nc.vector.scalar_tensor_tensor(
                 out=diffs[h, b][:, t, :], in0=level[:], scalar=gain_size[:, b, t : t + 1], in1=size[:],
                 op0=ALU.mult, op1=ALU.subtract,
             )
 
-        def finish_h(h, b, c):
-            width = HALF // 2
-            cols = slice(c * width, (c + 1) * width)
-            if c == 0:
-                h_codes[h, b] = keep.tile([P, HALF], U32, name="h_codes%d_%d" % (h, b), align_bytes=64)
-                h_planes[h, b] = keep.tile([P, HALF], U8, name="h_plane%d_%d" % (h, b), align_bytes=64)
-            woven = work.tile([P, width * PACK], BF16, name="woven", bufs=3, align_bytes=64)
-            nc.scalar.activation(
-                woven[:].rearrange("p (c i t) -> p c t i", i=4, t=PACK),
-                diffs[h, b][:, :, cols].rearrange("p t (c i) -> p c t i", i=4),
-                ACT.Abs,
+        def weave_views(woven, slices):
+            dst = woven[:].rearrange("p (c i t) -> p c t i", i=NEIGHBOURS, t=PACK)
+            src = slices.rearrange("p t (c i) -> p c t i", i=NEIGHBOURS)
+            return dst, src
+
+        def quantize_h(h, b, c0, woven):
+            if c0 == 0:
+                h_codes[h, b] = keep.tile([P, BANK], U32, name="h_codes%d_%d" % (h, b), align_bytes=64)
+                h_planes[h, b] = keep.tile([P, BANK], U8, name="h_plane%d_%d" % (h, b), align_bytes=64)
+            columns = slice(c0, c0 + PIECE)
+            dst, src = weave_views(woven, diffs[h, b][:, :, columns])
+            nc.scalar.activation(dst, src, ACT.Abs)
+            nc.vector.quantize_mx(
+                out=h_codes[h, b][:, columns].bitcast(FP8X4), scales=h_planes[h, b][:, columns], in_=woven[:]
             )
-            nc.vector.quantize_mx(out=h_codes[h, b][:, cols].bitcast(FP8X4), scales=h_planes[h, b][:, cols], in_=woven[:])
 
         def second_stage(h, t):
             u, e = divmod(t, 2)
-            cols = slice(e * P, (e + 1) * P)
-            acc = psum.tile([P, HALF], F32, name="acc", bufs=2)
+            acc = psum.tile([P, BANK], F32, name="acc", bufs=2)
             for b in range(PASSES):
+                codes, plane = w3_mx[b, u]
                 nc.tensor.matmul_mx(
-                    out=acc[:], lhsT=w3_codes[b, u][:, cols].bitcast(FP8X4), lhsT_scale=w3_planes[b, u][:, cols],
+                    out=acc[:], lhsT=codes[:, e * P : (e + 1) * P].bitcast(FP8X4), lhsT_scale=plane[:, e * P : (e + 1) * P],
                     rhs=h_codes[h, b][:].bitcast(FP8X4), rhs_scale=h_planes[h, b][:],
                     start=(b == 0), stop=(b == PASSES - 1),
                 )
-            nc.scalar.activation(g2[t][:, h * HALF : (h + 1) * HALF], acc[:], ACT.Silu)
+            nc.scalar.activation(g2[t][:, h * BANK : (h + 1) * BANK], acc[:], ACT.Silu)
 
-        between = {
-            (0, 1): [lambda: prep_w1(1, True), lambda: load_w3(1)],
-            (0, 3): [lambda: gather_words(1)],
-            (1, 1): [lambda: prep_w1(2, False), lambda: load_w3(2)],
-            (2, 2): [lambda: start_w3(0, 0)],
-            (2, 3): [lambda: end_w3(0, 0)],
-            (3, 2): [lambda: start_w3(1, 0)],
-            (3, 3): [lambda: end_w3(1, 0)],
-            (4, 2): [lambda: start_w3(2, 0)],
-            (4, 3): [lambda: end_w3(2, 0)],
-            (5, 1): [lambda: second_stage(0, 0)],
-            (5, 2): [lambda: start_w3(0, 1)],
-            (5, 3): [lambda: end_w3(0, 1)],
-        }
+        def size_tile():
+            return work.tile([P, BANK], F32, name="size", bufs=4)
+
+        def woven_tile(name):
+            return work.tile([P, PIECE * PACK], BF16, name=name, align_bytes=64)
+
         groups = [(h, b) for h in range(HALVES) for b in range(PASSES)]
+        w3_pairs = [(b, u) for u in range(2) for b in range(PASSES)]
+        first_w3_group = PASSES - 1
+        last_size = keep.tile([P, BANK], F32, name="last_size", tag="after_last_diff", align_bytes=64)
         for g, (h, b) in enumerate(groups):
             for t in range(PACK):
-                first_stage(h, b, t)
-                if g > 0 and t < 2:
-                    finish_h(*groups[g - 1], t)
-                for job in between.get((g, t), []):
-                    job()
-        for c in range(2):
-            finish_h(*groups[-1], c)
-        second_stage(1, 0)
-        for b in (1, 2):
-            start_w3(b, 1)
-        for b in (1, 2):
-            end_w3(b, 1)
-        for t in range(1, PACK):
+                is_last = g == len(groups) - 1 and t == PACK - 1
+                first_stage(h, b, t, last_size if is_last else size_tile())
+                if g > 0 and t * PIECE < BANK:
+                    quantize_h(*groups[g - 1], t * PIECE, woven_tile("h_woven"))
+                if g == 0 and t == 1:
+                    prepare_w1(1, (on_vector, on_scalar))
+                    load_w3(0)
+                    load_w3(1)
+                if g == 1 and t == 1:
+                    prepare_w1(2, (on_vector, on_vector))
+                    load_w3(2)
+                if g >= first_w3_group and t == 2:
+                    weave_w3(*w3_pairs[g - first_w3_group], woven_tile("w3_woven"))
+                if g >= first_w3_group and t == 3:
+                    quantize_w3(*w3_pairs[g - first_w3_group])
+
+        last_woven = keep.tile([P, PIECE * PACK], BF16, name="last_woven", tag="after_last_weave", align_bytes=64)
+        quantize_h(*groups[-1], 0, woven_tile("h_woven"))
+        quantize_h(*groups[-1], PIECE, last_woven)
+        for t in range(2):
+            for h in range(HALVES):
+                second_stage(h, t)
+        for pair, tag in zip(w3_pairs[-2:], ("after_last_diff", "after_last_weave")):
+            weave_w3(*pair, keep.tile([P, PIECE * PACK], BF16, name="w3_late", tag=tag, align_bytes=64))
+            quantize_w3(*pair)
+        for t in range(2, PACK):
             for h in range(HALVES):
                 second_stage(h, t)
 
@@ -254,39 +261,40 @@ def tile_list_plank_pair_features_kernel(
         out_words = out_1[0].rearrange("p m t -> p (m t)").bitcast(I32)
 
         def pick_beside(t, c0, c1):
-            other = work.tile([P, c1 - c0], F32, name="other", bufs=3)
-            weighted = work.tile([P, c1 - c0], F32, name="weighted", bufs=3)
-            nc.vector.tensor_copy(other[:], g2[t][:].indirect(pos2_sb[:, c0 // LIST_ROWS : c1 // LIST_ROWS]))
+            other = work.tile([P, c1 - c0], F32, name="other")
+            weighted = work.tile([P, c1 - c0], F32, name="weighted")
+            nc.vector.tensor_copy(other[:], g2[t][:].indirect(pos2_sb[:, c0 // STRIPE : c1 // STRIPE]))
             nc.scalar.activation(weighted[:], other[:], ACT.Copy, scale=beside_sb[:, t : t + 1])
             return weighted
 
         def pick_own(t, c0, c1, weighted):
-            nc.vector.tensor_tensor(
-                y[:, t, c0:c1], g2[t][:].indirect(pos1_sb[:, c0 // LIST_ROWS : c1 // LIST_ROWS]), weighted[:], ALU.add
-            )
-            nc.sync.dma_start(out=out_rows[:, t, c0:c1], in_=y[:, t, c0:c1])
+            own = g2[t][:].indirect(pos1_sb[:, c0 // STRIPE : c1 // STRIPE])
+            nc.vector.tensor_tensor(y[:, t, c0:c1], own, weighted[:], ALU.add)
 
-        def planes_of(c0, c1, on_scalar):
-            woven = work.tile([P, (c1 - c0) * PACK], BF16, name="y_woven", bufs=2, align_bytes=64)
-            dst = woven[:].rearrange("p (c i t) -> p c t i", i=4, t=PACK)
-            src = y[:, :, c0:c1].rearrange("p t (c i) -> p c t i", i=4)
-            if on_scalar:
-                nc.scalar.copy(out=dst, in_=src)
-            else:
-                nc.vector.tensor_copy(out=dst, in_=src)
+        def store_planes(c0, c1, copy):
+            woven = work.tile([P, (c1 - c0) * PACK], BF16, name="y_woven", align_bytes=64)
+            dst, src = weave_views(woven, y[:, :, c0:c1])
+            copy(out=dst, in_=src)
             nc.vector.quantize_mx(out=y_codes[:, c0:c1].bitcast(FP8X4), scales=y_plane[:, c0:c1], in_=woven[:])
             nc.scalar.dma_start(out=out_words[:, c0:c1], in_=y_codes[:, c0:c1].bitcast(I32))
 
-        pieces = [(0, 0, M), (1, 0, M), (2, 0, M), (3, 0, M // 2), (3, M // 2, M)]
+        last_cuts = (0, PIECE, PIECE + PIECE // 2, M)
+        pieces = [(t, c0, c0 + PIECE) for t in range(PACK - 1) for c0 in range(0, M, PIECE)]
+        pieces = pieces + [(PACK - 1, c0, c1) for c0, c1 in zip(last_cuts, last_cuts[1:])]
         weighted = pick_beside(*pieces[0])
-        for i, piece in enumerate(pieces):
+        for i, (t, c0, c1) in enumerate(pieces):
             ahead = pick_beside(*pieces[i + 1]) if i + 1 < len(pieces) else None
-            pick_own(*piece, weighted)
+            pick_own(t, c0, c1, weighted)
             weighted = ahead
-        planes_of(0, M // 2, True)
-        planes_of(M // 2, M, False)
-        for q in range(4):
+            if t == PACK - 1:
+                nc.sync.dma_start(out=out_rows[:, t, c0:c1], in_=y[:, t, c0:c1])
+                store_planes(c0, c1, on_scalar if c1 < M else on_vector)
+            elif c1 == M:
+                nc.sync.dma_start(out=out_rows[:, t, :], in_=y[:, t, :])
+
+        for q in range(P // QUADRANT):
             queue = nc.sync if q % 2 == 0 else nc.scalar
             queue.dma_start(
-                out=out_2[0, 4 * q : 4 * q + 4, :].bitcast(I32), in_=y_plane[32 * q : 32 * q + 4, :].bitcast(I32)
+                out=out_2[0, 4 * q : 4 * q + 4, :].bitcast(I32),
+                in_=y_plane[QUADRANT * q : QUADRANT * q + 4, :].bitcast(I32),
             )

@@ -158,9 +158,9 @@ def tile_list_plank_pair_features_kernel(
         nc.scalar.activation(gain_size[:], gain_sb[:], ACT.Abs)
 
         h_codes, h_planes, diffs = {}, {}, {}
-        g2 = [keep.tile([P, S], F32, name="g2_%d" % t) for t in range(PACK)]
+        g2 = {}
 
-        def first_stage(h, b, t, size):
+        def first_stage(h, b, t, size, diff):
             u, e = divmod(t, 2)
             codes, plane = w1_mx[b, u]
             moving = picked[h][:].bitcast(FP8X4)
@@ -178,10 +178,8 @@ def tile_list_plank_pair_features_kernel(
                 rhs=moving, rhs_scale=moving_plane, start=True, stop=True,
             )
             nc.scalar.activation(size[:], stripe[:], ACT.Abs, scale=gain_sb[:, b, t : t + 1])
-            if t == 0:
-                diffs[h, b] = work.tile([P, PACK, BANK], BF16, name="diff")
             nc.vector.scalar_tensor_tensor(
-                out=diffs[h, b][:, t, :], in0=level[:], scalar=gain_size[:, b, t : t + 1], in1=size[:],
+                out=diff[:, t, :], in0=level[:], scalar=gain_size[:, b, t : t + 1], in1=size[:],
                 op0=ALU.mult, op1=ALU.subtract,
             )
 
@@ -223,13 +221,15 @@ def tile_list_plank_pair_features_kernel(
         w3_pairs = [(b, u) for u in range(2) for b in range(PASSES)]
         first_w3_group = PASSES - 1
         last_size = keep.tile([P, BANK], F32, name="last_size", tag="after_last_diff", align_bytes=64)
+        last_diff = keep.tile([P, PACK, BANK], BF16, name="last_diff", tag="after_last_group")
         for g, (h, b) in enumerate(groups):
+            is_last = g == len(groups) - 1
+            diffs[h, b] = last_diff if is_last else work.tile([P, PACK, BANK], BF16, name="diff")
             for t in range(PACK):
-                is_last = g == len(groups) - 1 and t == PACK - 1
-                first_stage(h, b, t, last_size if is_last else size_tile())
-                if g > 0 and t * PIECE < BANK:
-                    quantize_h(*groups[g - 1], t * PIECE, woven_tile("h_woven"))
-                if g == 0 and t == 1:
+                first_stage(h, b, t, last_size if is_last and t == PACK - 1 else size_tile(), diffs[h, b])
+                if g > 0 and t % 2 == 1:
+                    quantize_h(*groups[g - 1], t // 2 * PIECE, woven_tile("h_woven"))
+                if g == 0 and t == 3:
                     prepare_w1(1, (on_vector, on_scalar))
                     load_w3(0)
                     load_w3(1)
@@ -244,6 +244,8 @@ def tile_list_plank_pair_features_kernel(
         last_woven = keep.tile([P, PIECE * PACK], BF16, name="last_woven", tag="after_last_weave", align_bytes=64)
         quantize_h(*groups[-1], 0, woven_tile("h_woven"))
         quantize_h(*groups[-1], PIECE, last_woven)
+        for t in range(PACK):
+            g2[t] = keep.tile([P, S], F32, name="g2_%d" % t, tag="after_last_group" if t == 0 else "g2_%d" % t)
         for t in range(2):
             for h in range(HALVES):
                 second_stage(h, t)

@@ -85,11 +85,10 @@ def tile_list_plank_pair_features_kernel(
 
         picked_scales = keep.tile([P, S], U8, name="picked_scales", tag="a")
         staged = keep.tile([P, S + H], U8, name="staged", tag="b")
-        for b in range(PASSES):
-            nc.vector.tensor_copy(
-                out=staged[:, S + b * PASS : S + (b + 1) * PASS].rearrange("p (t m) -> p t m", t=PACK),
-                in_=w4_raw_scales[:, b * PASS : (b + 1) * PASS].rearrange("p (m t) -> p t m", t=PACK),
-            )
+        nc.vector.tensor_copy(
+            out=staged[:, S:].rearrange("p (b t m) -> p b t m", b=PASSES, t=PACK),
+            in_=w4_raw_scales[:].rearrange("p (b m t) -> p b t m", b=PASSES, t=PACK),
+        )
         nc.vector.tensor_copy(picked_scales[:], table_scales[:].indirect(offs_sb[:]))
         nc.vector.tensor_copy(out=staged[:, 0:S].bitcast(I32), in_=picked_scales[:].bitcast(I32))
         for q in range(P // QUADRANT):
@@ -184,20 +183,19 @@ def tile_list_plank_pair_features_kernel(
             )
 
         def weave_views(woven, slices):
-            dst = woven[:].rearrange("p (c i t) -> p c t i", i=NEIGHBOURS, t=PACK)
+            dst = woven.rearrange("p (c i t) -> p c t i", i=NEIGHBOURS, t=PACK)
             src = slices.rearrange("p t (c i) -> p c t i", i=NEIGHBOURS)
             return dst, src
 
-        def quantize_h(h, b, c0, woven):
+        def weave_h(h, b, c0, woven):
+            dst, src = weave_views(woven, diffs[h, b][:, :, c0 : c0 + PIECE])
+            nc.scalar.activation(dst, src, ACT.Abs)
+
+        def quantize_h(h, b, c0, c1, woven):
             if c0 == 0:
                 h_codes[h, b] = keep.tile([P, BANK], U32, name="h_codes%d_%d" % (h, b), align_bytes=64)
                 h_planes[h, b] = keep.tile([P, BANK], U8, name="h_plane%d_%d" % (h, b), align_bytes=64)
-            columns = slice(c0, c0 + PIECE)
-            dst, src = weave_views(woven, diffs[h, b][:, :, columns])
-            nc.scalar.activation(dst, src, ACT.Abs)
-            nc.vector.quantize_mx(
-                out=h_codes[h, b][:, columns].bitcast(FP8X4), scales=h_planes[h, b][:, columns], in_=woven[:]
-            )
+            nc.vector.quantize_mx(out=h_codes[h, b][:, c0:c1].bitcast(FP8X4), scales=h_planes[h, b][:, c0:c1], in_=woven)
 
         def second_stage(h, t):
             u, e = divmod(t, 2)
@@ -227,8 +225,12 @@ def tile_list_plank_pair_features_kernel(
             diffs[h, b] = last_diff if is_last else work.tile([P, PACK, BANK], BF16, name="diff")
             for t in range(PACK):
                 first_stage(h, b, t, last_size if is_last and t == PACK - 1 else size_tile(), diffs[h, b])
-                if g > 0 and t % 2 == 1:
-                    quantize_h(*groups[g - 1], t // 2 * PIECE, woven_tile("h_woven"))
+                if g > 0 and t == 1:
+                    h_woven = work.tile([P, BANK * PACK], BF16, name="h_woven", bufs=2, align_bytes=64)
+                    weave_h(*groups[g - 1], 0, h_woven[:, : PIECE * PACK])
+                if g > 0 and t == 3:
+                    weave_h(*groups[g - 1], PIECE, h_woven[:, PIECE * PACK :])
+                    quantize_h(*groups[g - 1], 0, BANK, h_woven[:])
                 if g == 0 and t == 3:
                     prepare_w1(1, (on_vector, on_scalar))
                     load_w3(0)
@@ -242,8 +244,9 @@ def tile_list_plank_pair_features_kernel(
                     quantize_w3(*w3_pairs[g - first_w3_group])
 
         last_woven = keep.tile([P, PIECE * PACK], BF16, name="last_woven", tag="after_last_weave", align_bytes=64)
-        quantize_h(*groups[-1], 0, woven_tile("h_woven"))
-        quantize_h(*groups[-1], PIECE, last_woven)
+        for c0, woven in ((0, woven_tile("last_but_one_woven")), (PIECE, last_woven)):
+            weave_h(*groups[-1], c0, woven[:])
+            quantize_h(*groups[-1], c0, c0 + PIECE, woven[:])
         for t in range(PACK):
             g2[t] = keep.tile([P, S], F32, name="g2_%d" % t, tag="after_last_group" if t == 0 else "g2_%d" % t)
         for t in range(2):
@@ -270,12 +273,17 @@ def tile_list_plank_pair_features_kernel(
             return weighted
 
         def pick_own(t, c0, c1, weighted):
-            own = g2[t][:].indirect(pos1_sb[:, c0 // STRIPE : c1 // STRIPE])
-            nc.vector.tensor_tensor(y[:, t, c0:c1], own, weighted[:], ALU.add)
+            looked_up = g2[t][:].indirect(pos1_sb[:, c0 // STRIPE : c1 // STRIPE])
+            if t == PACK - 1:
+                nc.vector.tensor_tensor(y[:, t, c0:c1], looked_up, weighted[:], ALU.add)
+            else:
+                own = work.tile([P, c1 - c0], F32, name="own")
+                nc.vector.tensor_copy(own[:], looked_up)
+                nc.gpsimd.tensor_tensor(y[:, t, c0:c1], own[:], weighted[:], ALU.add)
 
         def store_planes(c0, c1, copy):
             woven = work.tile([P, (c1 - c0) * PACK], BF16, name="y_woven", align_bytes=64)
-            dst, src = weave_views(woven, y[:, :, c0:c1])
+            dst, src = weave_views(woven[:], y[:, :, c0:c1])
             copy(out=dst, in_=src)
             nc.vector.quantize_mx(out=y_codes[:, c0:c1].bitcast(FP8X4), scales=y_plane[:, c0:c1], in_=woven[:])
             nc.scalar.dma_start(out=out_words[:, c0:c1], in_=y_codes[:, c0:c1].bitcast(I32))

@@ -58,10 +58,6 @@ def tile_list_plank_pair_features_kernel(
         nc.vector.memset(table_scales[:].bitcast(I32), 0)
         nc.vector.memset(planes[:].bitcast(I32), 0)
 
-        warm = keep.tile([P, 2], F32, name="warm")
-        nc.vector.memset(warm[:, 0:1], 0.0)
-        nc.scalar.activation(warm[:, 1:2], warm[:, 0:1], ACT.Silu)
-
         def load_w1(b):
             w1_raw[b] = keep.tile([P, PACK, PASS], F32, name="w1_raw%d" % b, tag=w1_tags[b])
             columns = w1[:, b * PASS : (b + 1) * PASS]
@@ -85,10 +81,11 @@ def tile_list_plank_pair_features_kernel(
 
         picked_scales = keep.tile([P, S], U8, name="picked_scales", tag="a")
         staged = keep.tile([P, S + H], U8, name="staged", tag="b")
-        nc.vector.tensor_copy(
-            out=staged[:, S:].rearrange("p (b t m) -> p b t m", b=PASSES, t=PACK),
-            in_=w4_raw_scales[:].rearrange("p (b m t) -> p b t m", b=PASSES, t=PACK),
-        )
+        for b in range(PASSES):
+            nc.vector.tensor_copy(
+                out=staged[:, S + b * PASS : S + (b + 1) * PASS].rearrange("p (t m) -> p t m", t=PACK),
+                in_=w4_raw_scales[:, b * PASS : (b + 1) * PASS].rearrange("p (m t) -> p t m", t=PACK),
+            )
         nc.vector.tensor_copy(picked_scales[:], table_scales[:].indirect(offs_sb[:]))
         nc.vector.tensor_copy(out=staged[:, 0:S].bitcast(I32), in_=picked_scales[:].bitcast(I32))
         for q in range(P // QUADRANT):
@@ -155,6 +152,10 @@ def tile_list_plank_pair_features_kernel(
         )
         nc.vector.tensor_scalar(out=sign[:], in0=sign_plus_one[:], scalar1=-1.0, scalar2=None, op0=ALU.add)
         nc.scalar.activation(gain_size[:], gain_sb[:], ACT.Abs)
+
+        beside_wide = [keep.tile([P, PIECE], F32, name="beside_wide%d" % t) for t in range(PACK)]
+        for t in range(PACK):
+            nc.scalar.copy(out=beside_wide[t][:], in_=beside_sb[:, t : t + 1].to_broadcast([P, PIECE]))
 
         h_codes, h_planes, diffs = {}, {}, {}
         g2 = {}
@@ -266,20 +267,14 @@ def tile_list_plank_pair_features_kernel(
         out_words = out_1[0].rearrange("p m t -> p (m t)").bitcast(I32)
 
         def pick_beside(t, c0, c1):
-            other = work.tile([P, c1 - c0], F32, name="other")
             weighted = work.tile([P, c1 - c0], F32, name="weighted")
-            nc.vector.tensor_copy(other[:], g2[t][:].indirect(pos2_sb[:, c0 // STRIPE : c1 // STRIPE]))
-            nc.scalar.activation(weighted[:], other[:], ACT.Copy, scale=beside_sb[:, t : t + 1])
+            other = g2[t][:].indirect(pos2_sb[:, c0 // STRIPE : c1 // STRIPE])
+            nc.vector.tensor_tensor(weighted[:], other, beside_wide[t][:, : c1 - c0], ALU.mult)
             return weighted
 
         def pick_own(t, c0, c1, weighted):
-            looked_up = g2[t][:].indirect(pos1_sb[:, c0 // STRIPE : c1 // STRIPE])
-            if t == PACK - 1:
-                nc.vector.tensor_tensor(y[:, t, c0:c1], looked_up, weighted[:], ALU.add)
-            else:
-                own = work.tile([P, c1 - c0], F32, name="own")
-                nc.vector.tensor_copy(own[:], looked_up)
-                nc.gpsimd.tensor_tensor(y[:, t, c0:c1], own[:], weighted[:], ALU.add)
+            own = g2[t][:].indirect(pos1_sb[:, c0 // STRIPE : c1 // STRIPE])
+            nc.vector.tensor_tensor(y[:, t, c0:c1], own, weighted[:], ALU.add)
 
         def store_planes(c0, c1, copy):
             woven = work.tile([P, (c1 - c0) * PACK], BF16, name="y_woven", align_bytes=64)

from contextlib import ExitStack

import concourse.mybir as mybir

K, H, N, T, S, M = 512, 1536, 512, 4096, 1024, 512
FLOPS = 2 * (2 * K * H * S + H * N * S)

F32 = mybir.dt.float32
BF16 = mybir.dt.bfloat16
I32 = mybir.dt.int32
U32 = mybir.dt.uint32
U16 = mybir.dt.uint16
U8 = mybir.dt.uint8
FP8X4 = mybir.dt.float8_e4m3fn_x4
FP4X4 = mybir.dt.float4_e2m1fn_x4
ALU = mybir.AluOpType
ACT = mybir.ActivationFunctionType

P = 128
PACK = 4
PASS = P * PACK
PASSES = H // PASS
BANK = 512
HALVES = S // BANK
BLOCKS = PASS // 32
QUADRANT = 32
STRIPE = 16
PIECE = 256
NEIGHBOURS = 4


def tile_list_plank_pair_features_kernel(
    tc, tab_words, tab_scales, offs, pos1, pos2, w1, w4_words, w4_scales, gain, w3, beside, out_0, out_1, out_2
):
    nc = tc.nc
    with ExitStack() as ctx:
        lists = ctx.enter_context(tc.tile_pool(name="lists", bufs=1))
        keep = ctx.enter_context(tc.tile_pool(name="keep", bufs=1))
        work = ctx.enter_context(tc.tile_pool(name="work", bufs=3))
        psum = ctx.enter_context(tc.psum_pool(name="psum", bufs=3))

        w1_tags = ("w1_first", "a", "b")
        w3_tags = ("c", "a", "b")

        offs_sb = lists.tile([P, S // STRIPE], U16, name="offs_sb")
        pos1_sb = lists.tile([P, M // STRIPE], U16, name="pos1_sb")
        pos2_sb = lists.tile([P, M // STRIPE], U16, name="pos2_sb")
        table = keep.tile([P, T], I32, name="table", tag="c")
        table_scales = keep.tile([P, T], U8, name="table_scales")
        w4_raw = keep.tile([P, 2 * H], U8, name="w4_raw")
        w4_raw_scales = keep.tile([P, H], U8, name="w4_raw_scales")
        gain_sb = keep.tile([P, PASSES, PACK], F32, name="gain_sb")
        beside_sb = keep.tile([P, PACK], F32, name="beside_sb")
        planes = keep.tile([P, S + H], U8, name="planes", align_bytes=64)
        w1_raw, w3_raw = {}, {}

        nc.gpsimd.memset(w4_raw_scales[:].bitcast(I32), 0)
        nc.vector.memset(table_scales[:].bitcast(I32), 0)
        nc.vector.memset(planes[:].bitcast(I32), 0)

        def load_w1(b):
            w1_raw[b] = keep.tile([P, PACK, PASS], F32, name="w1_raw%d" % b, tag=w1_tags[b])
            columns = w1[:, b * PASS : (b + 1) * PASS]
            nc.sync.dma_start(out=w1_raw[b][:], in_=columns.rearrange("(p j) c -> p j c", j=PACK))

        def load_w3(b):
            w3_raw[b] = keep.tile([P, PACK, N], F32, name="w3_raw%d" % b, tag=w3_tags[b])
            rows = w3[b * PASS : (b + 1) * PASS, :]
            nc.sync.dma_start(out=w3_raw[b][:], in_=rows.rearrange("(p j) n -> p j n", j=PACK))

        nc.sync.dma_start(offs_sb[:], offs)
        nc.sync.dma_start(out=w4_raw_scales[0:BLOCKS, :].bitcast(I32), in_=w4_scales[0].bitcast(I32))
        nc.sync.dma_start(out=table_scales[0:BLOCKS, :].bitcast(I32), in_=tab_scales[0].bitcast(I32))
        nc.sync.dma_start(out=gain_sb[:], in_=gain.rearrange("(b p t) -> p b t", p=P, t=PACK))
        nc.sync.dma_start(out=table[:], in_=tab_words[0].rearrange("p n t -> p (n t)").bitcast(I32))
        nc.sync.dma_start(out=beside_sb[:], in_=beside.rearrange("(p t) -> p t", t=PACK))
        nc.sync.dma_start(pos1_sb[:], pos1)
        load_w1(0)
        nc.sync.dma_start(out=w4_raw[:].bitcast(I32), in_=w4_words[0].bitcast(I32))
        nc.sync.dma_start(pos2_sb[:], pos2)

        picked_scales = keep.tile([P, S], U8, name="picked_scales", tag="a")
        staged = keep.tile([P, S + H], U8, name="staged", tag="b")
        for b in range(PASSES):
            nc.vector.tensor_copy(
                out=staged[:, S + b * PASS : S + (b + 1) * PASS].rearrange("p (t m) -> p t m", t=PACK),
                in_=w4_raw_scales[:, b * PASS : (b + 1) * PASS].rearrange("p (m t) -> p t m", t=PACK),
            )
        nc.vector.tensor_copy(picked_scales[:], table_scales[:].indirect(offs_sb[:]))
        nc.vector.tensor_copy(out=staged[:, 0:S].bitcast(I32), in_=picked_scales[:].bitcast(I32))
        for q in range(P // QUADRANT):
            nc.sync.dma_start(
                out=planes[QUADRANT * q : QUADRANT * q + 4, :].bitcast(I32), in_=staged[4 * q : 4 * q + 4, :].bitcast(I32)
            )
        load_w1(1)
        load_w1(2)

        picked = [keep.tile([P, BANK], U32, name="picked%d" % h, align_bytes=64) for h in range(HALVES)]
        w4_codes, w1_mx, w3_mx, w3_woven = {}, {}, {}, {}

        def gather_words(h):
            entries = offs_sb[:, h * BANK // STRIPE : (h + 1) * BANK // STRIPE]
            nc.vector.tensor_copy(picked[h][:], table[:].bitcast(U32).indirect(entries))

        def deal_w4(b):
            w4_codes[b] = keep.tile([P, 2 * PASS], U8, name="w4_codes%d" % b, align_bytes=64)
            nc.vector.tensor_copy(
                out=w4_codes[b][:].bitcast(U16).rearrange("p (t m) -> p t m", t=PACK),
                in_=w4_raw[:].bitcast(U16)[:, b * PASS : (b + 1) * PASS].rearrange("p (m t) -> p t m", t=PACK),
            )

        def dealt_views(woven, raw, u):
            src = raw[:].rearrange("p j (m u e) -> p u m j e", u=2, e=2)[:, u]
            dst = woven[:].rearrange("p (e m j) -> p m j e", e=2, j=PACK)
            return dst, src

        def quantize_weight(woven, name):
            codes = keep.tile([P, 2 * P], U32, name=name + "_codes", align_bytes=64)
            plane = keep.tile([P, 2 * P], U8, name=name + "_plane", align_bytes=64)
            nc.vector.quantize_mx(out=codes[:].bitcast(FP8X4), scales=plane[:], in_=woven[:])
            return codes, plane

        def prepare_w1(b, copies):
            woven = [work.tile([P, 2 * PASS], BF16, name="w1_woven", bufs=4, align_bytes=64) for u in range(2)]
            for u in range(2):
                dst, src = dealt_views(woven[u], w1_raw[b], u)
                copies[u](out=dst, in_=src)
            for u in range(2):
                w1_mx[b, u] = quantize_weight(woven[u], "w1_%d_%d" % (b, u))

        def weave_w3(b, u, woven):
            dst, src = dealt_views(woven, w3_raw[b], u)
            signs = sign[:, b].unsqueeze(1).unsqueeze(3).to_broadcast([P, P, PACK, 2])
            nc.vector.tensor_tensor(out=dst, in0=src, in1=signs, op=ALU.mult)
            w3_woven[b, u] = woven

        def quantize_w3(b, u):
            w3_mx[b, u] = quantize_weight(w3_woven[b, u], "w3_%d_%d" % (b, u))

        on_vector, on_scalar = nc.vector.tensor_copy, nc.scalar.copy
        gather_words(0)
        prepare_w1(0, (on_vector, on_scalar))
        for b in range(PASSES):
            deal_w4(b)
        gather_words(1)

        sign_plus_one = keep.tile([P, PASSES, PACK], F32, name="sign_plus_one")
        sign = keep.tile([P, PASSES, PACK], F32, name="sign")
        gain_size = keep.tile([P, PASSES, PACK], F32, name="gain_size")
        nc.vector.tensor_scalar(
            out=sign_plus_one[:], in0=gain_sb[:], scalar1=0.0, scalar2=2.0, op0=ALU.is_ge, op1=ALU.mult
        )
        nc.vector.tensor_scalar(out=sign[:], in0=sign_plus_one[:], scalar1=-1.0, scalar2=None, op0=ALU.add)
        nc.scalar.activation(gain_size[:], gain_sb[:], ACT.Abs)

        beside_wide = [keep.tile([P, PIECE], F32, name="beside_wide%d" % t) for t in range(PACK)]
        for t in range(PACK):
            nc.scalar.copy(out=beside_wide[t][:], in_=beside_sb[:, t : t + 1].to_broadcast([P, PIECE]))

        h_codes, h_planes, diffs = {}, {}, {}
        g2 = {}

        def first_stage(h, b, t, size, diff):
            u, e = divmod(t, 2)
            codes, plane = w1_mx[b, u]
            moving = picked[h][:].bitcast(FP8X4)
            moving_plane = planes[:, h * BANK : (h + 1) * BANK]
            w4_column = S + b * PASS + t * P
            stripe = psum.tile([P, BANK], F32, name="stripe")
            level = psum.tile([P, BANK], F32, name="level")
            nc.tensor.matmul_mx(
                out=stripe[:], lhsT=codes[:, e * P : (e + 1) * P].bitcast(FP8X4), lhsT_scale=plane[:, e * P : (e + 1) * P],
                rhs=moving, rhs_scale=moving_plane, start=True, stop=True,
            )
            nc.tensor.matmul_mx(
                out=level[:], lhsT=w4_codes[b][:, 2 * t * P : 2 * (t + 1) * P].bitcast(FP4X4),
                lhsT_scale=planes[:, w4_column : w4_column + P],
                rhs=moving, rhs_scale=moving_plane, start=True, stop=True,
            )
            nc.scalar.activation(size[:], stripe[:], ACT.Abs, scale=gain_sb[:, b, t : t + 1])
            nc.vector.scalar_tensor_tensor(
                out=diff[:, t, :], in0=level[:], scalar=gain_size[:, b, t : t + 1], in1=size[:],
                op0=ALU.mult, op1=ALU.subtract,
            )

        def weave_views(woven, slices):
            dst = woven.rearrange("p (c i t) -> p c t i", i=NEIGHBOURS, t=PACK)
            src = slices.rearrange("p t (c i) -> p c t i", i=NEIGHBOURS)
            return dst, src

        def weave_h(h, b, c0, woven):
            dst, src = weave_views(woven, diffs[h, b][:, :, c0 : c0 + PIECE])
            nc.scalar.activation(dst, src, ACT.Abs)

        def quantize_h(h, b, c0, c1, woven):
            if c0 == 0:
                h_codes[h, b] = keep.tile([P, BANK], U32, name="h_codes%d_%d" % (h, b), align_bytes=64)
                h_planes[h, b] = keep.tile([P, BANK], U8, name="h_plane%d_%d" % (h, b), align_bytes=64)
            nc.vector.quantize_mx(out=h_codes[h, b][:, c0:c1].bitcast(FP8X4), scales=h_planes[h, b][:, c0:c1], in_=woven)

        def second_stage(h, t):
            u, e = divmod(t, 2)
            acc = psum.tile([P, BANK], F32, name="acc", bufs=2)
            for b in range(PASSES):
                codes, plane = w3_mx[b, u]
                nc.tensor.matmul_mx(
                    out=acc[:], lhsT=codes[:, e * P : (e + 1) * P].bitcast(FP8X4), lhsT_scale=plane[:, e * P : (e + 1) * P],
                    rhs=h_codes[h, b][:].bitcast(FP8X4), rhs_scale=h_planes[h, b][:],
                    start=(b == 0), stop=(b == PASSES - 1),
                )
            nc.scalar.activation(g2[t][:, h * BANK : (h + 1) * BANK], acc[:], ACT.Silu)

        def size_tile():
            return work.tile([P, BANK], F32, name="size", bufs=4)

        def woven_tile(name):
            return work.tile([P, PIECE * PACK], BF16, name=name, align_bytes=64)

        groups = [(h, b) for h in range(HALVES) for b in range(PASSES)]
        w3_pairs = [(b, u) for u in range(2) for b in range(PASSES)]
        first_w3_group = PASSES - 1
        last_size = keep.tile([P, BANK], F32, name="last_size", tag="after_last_diff", align_bytes=64)
        last_diff = keep.tile([P, PACK, BANK], BF16, name="last_diff", tag="after_last_group")
        for g, (h, b) in enumerate(groups):
            is_last = g == len(groups) - 1
            diffs[h, b] = last_diff if is_last else work.tile([P, PACK, BANK], BF16, name="diff")
            for t in range(PACK):
                first_stage(h, b, t, last_size if is_last and t == PACK - 1 else size_tile(), diffs[h, b])
                if g > 0 and t == 1:
                    h_woven = work.tile([P, BANK * PACK], BF16, name="h_woven", bufs=2, align_bytes=64)
                    weave_h(*groups[g - 1], 0, h_woven[:, : PIECE * PACK])
                if g > 0 and t == 3:
                    weave_h(*groups[g - 1], PIECE, h_woven[:, PIECE * PACK :])
                    quantize_h(*groups[g - 1], 0, BANK, h_woven[:])
                if g == 0 and t == 3:
                    prepare_w1(1, (on_vector, on_scalar))
                    load_w3(0)
                    load_w3(1)
                if g == 1 and t == 1:
                    prepare_w1(2, (on_vector, on_vector))
                    load_w3(2)
                if g >= first_w3_group and t == 2:
                    weave_w3(*w3_pairs[g - first_w3_group], woven_tile("w3_woven"))
                if g >= first_w3_group and t == 3:
                    quantize_w3(*w3_pairs[g - first_w3_group])

        last_woven = keep.tile([P, PIECE * PACK], BF16, name="last_woven", tag="after_last_weave", align_bytes=64)
        for c0, woven in ((0, woven_tile("last_but_one_woven")), (PIECE, last_woven)):
            weave_h(*groups[-1], c0, woven[:])
            quantize_h(*groups[-1], c0, c0 + PIECE, woven[:])
        for t in range(PACK):
            g2[t] = keep.tile([P, S], F32, name="g2_%d" % t, tag="after_last_group" if t == 0 else "g2_%d" % t)
        for t in range(2):
            for h in range(HALVES):
                second_stage(h, t)
        for pair, tag in zip(w3_pairs[-2:], ("after_last_diff", "after_last_weave")):
            weave_w3(*pair, keep.tile([P, PIECE * PACK], BF16, name="w3_late", tag=tag, align_bytes=64))
            quantize_w3(*pair)
        for t in range(2, PACK):
            for h in range(HALVES):
                second_stage(h, t)

        y = keep.tile([P, PACK, M], F32, name="y")
        y_codes = keep.tile([P, M], U32, name="y_codes", align_bytes=64)
        y_plane = keep.tile([P, M], U8, name="y_plane", align_bytes=64)
        out_rows = out_0.rearrange("(p t) m -> p t m", t=PACK)
        out_words = out_1[0].rearrange("p m t -> p (m t)").bitcast(I32)

        def pick_beside(t, c0, c1):
            weighted = work.tile([P, c1 - c0], F32, name="weighted")
            other = g2[t][:].indirect(pos2_sb[:, c0 // STRIPE : c1 // STRIPE])
            nc.vector.tensor_tensor(weighted[:], other, beside_wide[t][:, : c1 - c0], ALU.mult)
            return weighted

        def pick_own(t, c0, c1, weighted):
            own = g2[t][:].indirect(pos1_sb[:, c0 // STRIPE : c1 // STRIPE])
            nc.vector.tensor_tensor(y[:, t, c0:c1], own, weighted[:], ALU.add)

        def store_planes(c0, c1, copy):
            woven = work.tile([P, (c1 - c0) * PACK], BF16, name="y_woven", align_bytes=64)
            dst, src = weave_views(woven[:], y[:, :, c0:c1])
            copy(out=dst, in_=src)
            nc.vector.quantize_mx(out=y_codes[:, c0:c1].bitcast(FP8X4), scales=y_plane[:, c0:c1], in_=woven[:])
            nc.scalar.dma_start(out=out_words[:, c0:c1], in_=y_codes[:, c0:c1].bitcast(I32))

        last_cuts = (0, PIECE, PIECE + PIECE // 2, M)
        pieces = [(t, c0, c0 + PIECE) for t in range(PACK - 1) for c0 in range(0, M, PIECE)]
        pieces = pieces + [(PACK - 1, c0, c1) for c0, c1 in zip(last_cuts, last_cuts[1:])]
        weighted = pick_beside(*pieces[0])
        for i, (t, c0, c1) in enumerate(pieces):
            ahead = pick_beside(*pieces[i + 1]) if i + 1 < len(pieces) else None
            pick_own(t, c0, c1, weighted)
            weighted = ahead
            if t == PACK - 1:
                nc.sync.dma_start(out=out_rows[:, t, c0:c1], in_=y[:, t, c0:c1])
                store_planes(c0, c1, on_scalar if c1 < M else on_vector)
            elif c1 == M:
                nc.sync.dma_start(out=out_rows[:, t, :], in_=y[:, t, :])

        for q in range(P // QUADRANT):
            queue = nc.sync if q % 2 == 0 else nc.scalar
            queue.dma_start(
                out=out_2[0, 4 * q : 4 * q + 4, :].bitcast(I32),
                in_=y_plane[QUADRANT * q : QUADRANT * q + 4, :].bitcast(I32),
            )
